import numpy as np
import ml_dtypes


def mxq(x, axis, fmt="e4m3"):
    dtype, down = {"e4m3": (ml_dtypes.float8_e4m3fn, 7), "e5m2": (ml_dtypes.float8_e5m2, 14)}[fmt]
    v = np.moveaxis(np.asarray(x, np.float32).astype(ml_dtypes.bfloat16).astype(np.float64), axis, -1)
    blocks = v.reshape(v.shape[:-1] + (-1, 32))
    amax = np.abs(blocks).max(-1, keepdims=True)
    byte = np.maximum(np.where(amax > 0, np.frexp(amax)[1] - 1 + 127, 0) - down, 1)
    scale = np.exp2(byte - 127.0)
    codes = (blocks / scale).astype(np.float32).astype(dtype).astype(np.float64)
    return np.moveaxis((codes * scale).reshape(v.shape), -1, axis)


WIDE = False


def mx_kscale(k):
    if not WIDE:
        return np.ones(k)
    levels = np.array([10, -10, 5, -5, 0])
    if k % 512:
        return np.exp2(np.random.permutation(np.resize(levels, k // 32))).repeat(32)
    a = np.empty((k // 512, 16))
    for p in range(k // 512):
        a[p, :8] = np.random.permutation(np.resize(levels, 8))
        for g in range(8):
            far = levels[np.abs(levels - a[p, g]) >= 10]
            a[p, g + 8] = far[np.random.randint(len(far))]
    return np.exp2(a.ravel()).repeat(32)


def f64(x):
    return np.asarray(x).astype(np.float64)


def striped(idx):
    return np.tile(idx.reshape(-1, 16).T, (8, 1)).astype(np.uint16)


def unstriped(offs):
    return offs[:16].T.reshape(-1).astype(np.int64)


def striped8(idx):
    return np.concatenate([x.reshape(-1, 16).T for x in idx]).astype(np.uint16)


def runs(offs, k):
    lists = np.stack([offs[16 * r : 16 * r + 16].T.reshape(-1) for r in range(8)]).astype(np.int64)
    return lists[np.arange(k) % 512 // 64]


def pack_weight(w):
    k, n = w.shape
    w = f64(np.asarray(w, np.float32).astype(ml_dtypes.bfloat16)).reshape(k // 32, 32, n)
    amax = np.abs(w).max(1)
    byte = np.clip(np.where(amax > 0, np.frexp(amax)[1] - 1 + 127 - 7, 1), 1, 254)
    scaled = (w * np.exp2(127.0 - byte)[:, None, :]).reshape(k, n).astype(np.float32)
    words = np.ascontiguousarray(scaled.reshape(k // 512, 128, 4, n).transpose(0, 1, 3, 2)).astype(ml_dtypes.float8_e4m3fn).view(np.uint8)
    return words, np.ascontiguousarray(byte.astype(np.uint8).reshape(k // 512, 16, n))


def unpack_weight(words, scales):
    g, p, n, _ = words.shape
    vals = np.ascontiguousarray(words).view(ml_dtypes.float8_e4m3fn).astype(np.float64) * np.repeat(np.exp2(scales.astype(np.float64) - 127.0), 8, axis=1)[..., None]
    return vals.transpose(0, 1, 3, 2).reshape(g * 512, n)


E2M1 = np.array([0.0, 0.5, 1.0, 1.5, 2.0, 3.0, 4.0, 6.0, -0.0, -0.5, -1.0, -1.5, -2.0, -3.0, -4.0, -6.0])


def pack_fp4(w):
    k, n = w.shape
    w = f64(np.asarray(w, np.float32).astype(ml_dtypes.bfloat16)).reshape(k // 32, 32, n)
    amax = np.abs(w).max(1)
    mant, ex = np.frexp(amax / 6.0)
    byte = np.clip(np.where(amax > 0, np.where(mant > 0.5, ex, ex - 1) + 127, 1), 1, 254)
    scaled = (w * np.exp2(127.0 - byte)[:, None, :]).reshape(k, n).astype(np.float32)
    c = np.ascontiguousarray(scaled.reshape(k // 512, 128, 4, n).transpose(0, 1, 3, 2)).astype(ml_dtypes.float4_e2m1fn).view(np.uint8) & 0xF
    words = (c[..., 0::2] | (c[..., 1::2] << 4)).reshape(k // 512, 128, 2 * n)
    return np.ascontiguousarray(words), np.ascontiguousarray(byte.astype(np.uint8).reshape(k // 512, 16, n))


def unpack_fp4(words, scales):
    g, _, n = scales.shape
    words = np.ascontiguousarray(words).reshape(g, 128, n, 2)
    nib = np.empty((g, 128, n, 4), np.uint8)
    nib[..., 0::2] = words & 0xF
    nib[..., 1::2] = words >> 4
    vals = E2M1[nib] * np.repeat(np.exp2(scales.astype(np.float64) - 127.0), 8, axis=1)[..., None]
    return vals.transpose(0, 1, 3, 2).reshape(g * 512, n)


def planes(y):
    n, m = y.shape
    v = y.astype(np.float32).astype(ml_dtypes.bfloat16).astype(np.float64).reshape(n // 32, 32, m)
    top = np.abs(v).max(1)
    byte = np.clip(np.where(top > 0, np.frexp(top)[1] - 1 + 127 - 7, 1), 1, 254)
    codes = (v * np.exp2(127.0 - byte)[:, None, :]).reshape(n, m).astype(np.float32).astype(ml_dtypes.float8_e4m3fn).view(np.uint8)
    words = codes.reshape(n // 512, 128, 4, m).transpose(0, 1, 3, 2)
    return np.ascontiguousarray(words), np.ascontiguousarray(byte.astype(np.uint8).reshape(n // 512, 16, m))


K, T, S, N, H = 512, 2048, 512, 512, 512


def setup_inputs():
    n = np.random.standard_normal
    s = mx_kscale(K)[:, None]
    u = mx_kscale(H)
    packed_xT = pack_weight(n((K, T)) * s)
    packed_w1 = pack_fp4(n((K, H)) / np.sqrt(K) / s)
    packed_w2 = pack_fp4(n((H, N)) / np.sqrt(H) / u[:, None])
    packed_w3 = pack_fp4(n((K, N)) / np.sqrt(K) / s)
    return {
        "x_words": packed_xT[0],
        "x_scales": packed_xT[1],
        "w1_words": packed_w1[0],
        "w1_scales": packed_w1[1],
        "gn": (np.random.uniform(0.5, 1.5, (H, 1)) * u[:, None]).astype(np.float32),
        "w2_words": packed_w2[0],
        "w2_scales": packed_w2[1],
        "w3_words": packed_w3[0],
        "w3_scales": packed_w3[1],
        "offs": striped(np.random.permutation(T)[:S]),
        "n1": striped8(np.stack([np.random.permutation(S) for _ in range(8)])),
        "n2": striped8(np.stack([np.random.permutation(S) for _ in range(8)])),
        "two": striped(np.random.permutation(T)[:S]),
        "n3": striped8(np.stack([np.random.permutation(S) for _ in range(8)])),
        "n4": striped8(np.stack([np.random.permutation(S) for _ in range(8)])),
    }


def reference(x_words, x_scales, w1_words, w1_scales, gn, w2_words, w2_scales, w3_words, w3_scales, offs, n1, n2, two, n3, n4):
    xq = unpack_weight(x_words, x_scales)[:, unstriped(offs)]
    y = unpack_fp4(w1_words, w1_scales).T @ xq
    sq = (y) ** 2
    z = f64(gn) * ((y[np.arange(H)[:, None], runs(n2, H)]) / (np.sqrt(sq + sq[np.arange(H)[:, None], runs(n1, H)] + 0.25)))
    h = unpack_fp4(w2_words, w2_scales).T @ mxq(z, 0, "e4m3")
    x_two = unpack_weight(x_words, x_scales)[:, unstriped(two)]
    d = unpack_fp4(w3_words, w3_scales).T @ x_two
    out_0 = np.maximum(h, d[np.arange(N)[:, None], runs(n4, N)]) - (np.minimum(h[np.arange(N)[:, None], runs(n3, N)], d))
    return (out_0,) + planes(out_0)

@@ -1,0 +1,177 @@
+from contextlib import ExitStack
+
+import concourse.mybir as mybir
+
+K, T, S, N, H = 512, 2048, 512, 512, 512
+FLOPS = 3 * 2 * 512 * 512 * 512
+
+F32 = mybir.dt.float32
+BF16 = mybir.dt.bfloat16
+I32 = mybir.dt.int32
+U32 = mybir.dt.uint32
+U16 = mybir.dt.uint16
+U8 = mybir.dt.uint8
+FP8X4 = mybir.dt.float8_e4m3fn_x4
+FP4X4 = mybir.dt.float4_e2m1fn_x4
+ALU = mybir.AluOpType
+ACT = mybir.ActivationFunctionType
+
+P = 128
+PACK = 4
+PIECES = ((0, 256), (256, 384), (384, 512))
+
+
+def tile_picked_latemaxbrms_none_po_kernel(tc, x_words, x_scales, w1_words, w1_scales, gn, w2_words, w2_scales, w3_words, w3_scales, offs, n1, n2, two, n3, n4, out_0, out_1, out_2):
+    nc = tc.nc
+    with ExitStack() as ctx:
+        lists = ctx.enter_context(tc.tile_pool(name="lists", bufs=1))
+        sb = ctx.enter_context(tc.tile_pool(name="sb", bufs=1))
+        ps = ctx.enter_context(tc.psum_pool(name="ps", bufs=1))
+
+        def tile(name, shape, dtype, tag=None):
+            return sb.tile(shape, dtype, name=name, tag=tag or name, align_bytes=64)
+
+        def load_list(name, src):
+            t = lists.tile([P, S // 16], U16, name=name)
+            nc.sync.dma_start(t[:], src)
+            return t
+
+        def scale_tile(name, width, engine):
+            t = tile(name, [P, width], U8)
+            engine.memset(t[:].bitcast(I32), 0)
+            return t
+
+        def load_scale_rows(t, src):
+            for q in range(4):
+                nc.sync.dma_start(t[32 * q : 32 * q + 4, :].bitcast(I32), src[0, 4 * q : 4 * q + 4, :].bitcast(I32))
+
+        def load_words(name, src):
+            t = tile(name, [P, 2 * N], U8)
+            nc.sync.dma_start(t[:].bitcast(I32), src[0].bitcast(I32))
+            return t
+
+        def deal(name, words, scales):
+            dw = tile(name + "_dw", [P, 2 * N], U8)
+            ds = tile(name + "_ds", [P, N], U8)
+            nc.vector.tensor_copy(dw[:].rearrange("p (t m b) -> p t m b", t=PACK, b=2), words[:].rearrange("p (m t b) -> p t m b", t=PACK, b=2))
+            nc.vector.tensor_copy(ds[:].rearrange("p (t m) -> p t m", t=PACK), scales[:].rearrange("p (m t) -> p t m", t=PACK))
+            return dw, ds
+
+        def product(bank, w, t, codes, scales):
+            dw, ds = w
+            nc.tensor.matmul_mx(
+                out=bank,
+                lhsT=dw[:, 2 * P * t : 2 * P * (t + 1)].bitcast(FP4X4),
+                lhsT_scale=ds[:, P * t : P * (t + 1)],
+                rhs=codes.bitcast(FP8X4),
+                rhs_scale=scales,
+                start=True,
+                stop=True,
+            )
+
+        def weave(copy, dst, src):
+            copy(dst.rearrange("p (c i t) -> p c t i", i=4, t=PACK), src.rearrange("p t (c i) -> p c t i", i=4))
+
+        xs = scale_tile("xs", T, nc.gpsimd)
+        w1s = scale_tile("w1s", N, nc.vector)
+        w3s = scale_tile("w3s", N, nc.vector)
+        w2s = scale_tile("w2s", N, nc.vector)
+        warm = tile("warm", [P, 2], F32)
+        nc.gpsimd.memset(warm[:, 0:1], 1.0)
+        nc.scalar.activation(warm[:, 1:2], warm[:, 0:1], ACT.Abs_reciprocal_sqrt)
+
+        offs_t = load_list("offs", offs)
+        two_t = load_list("two", two)
+        w1w = load_words("w1w", w1_words)
+        load_scale_rows(xs, x_scales)
+        xw = tile("xw", [P, T], I32)
+        nc.sync.dma_start(xw[:], x_words[0].rearrange("p n t -> p (n t)").bitcast(I32))
+        load_scale_rows(w1s, w1_scales)
+        w3w = load_words("w3w", w3_words)
+        w2w = load_words("w2w", w2_words)
+        n1_t = load_list("n1", n1)
+        load_scale_rows(w3s, w3_scales)
+        gain = tile("gain", [P, PACK], F32)
+        nc.sync.dma_start(gain[:], gn.rearrange("(p t) o -> p (t o)", t=PACK))
+        n2_t = load_list("n2", n2)
+        load_scale_rows(w2s, w2_scales)
+        n4_t = load_list("n4", n4)
+        n3_t = load_list("n3", n3)
+
+        def pick(name, table, dtype, lst):
+            picked = tile(name, [P, S], dtype)
+            nc.vector.tensor_copy(picked[:], table.indirect(lst[:]))
+            return picked
+
+        xa_s = pick("xa_s", xs[:], U8, offs_t)
+        w1 = deal("w1", w1w, w1s)
+        xa_w = pick("xa_w", xw[:].bitcast(U32), U32, offs_t)
+        y_ps = [ps.tile([P, S], F32, name=f"y{t}", tag=f"yh{t}") for t in range(PACK)]
+        for t in range(PACK):
+            product(y_ps[t][:], w1, t, xa_w[:], xa_s[:])
+        xb_s = pick("xb_s", xs[:], U8, two_t)
+        xb_w = pick("xb_w", xw[:].bitcast(U32), U32, two_t)
+        w3 = deal("w3", w3w, w3s)
+        w2 = deal("w2", w2w, w2s)
+        d_ps = [ps.tile([P, S], F32, name=f"d{t}") for t in range(PACK)]
+        for t in range(PACK):
+            product(d_ps[t][:], w3, t, xb_w[:], xb_s[:])
+
+        sq = [tile(f"sq{t}", [P, 2 * S], F32) for t in range(PACK)]
+        yg = [tile(f"yg{t}", [P, 2 * S], F32) for t in range(PACK)]
+        dw = [tile(f"dw{t}", [P, 2 * S], F32) for t in range(PACK)]
+        for t in range(PACK):
+            nc.scalar.activation(sq[t][:, :S], y_ps[t][:], ACT.Square)
+            nc.scalar.activation(sq[t ^ 1][:, S:], y_ps[t][:], ACT.Square)
+        for t in range(PACK):
+            nc.vector.tensor_tensor(yg[t][:, S:], sq[t][:].indirect(n1_t[:]), sq[t ^ 1][:, S:], ALU.add)
+        zf = tile("zf", [P, PACK, S], F32)
+        for t in range(PACK):
+            nc.scalar.activation(yg[t][:, :S], y_ps[t][:], ACT.Copy, scale=gain[:, t : t + 1])
+            nc.scalar.activation(dw[t][:, S:], yg[t][:, S:], ACT.Abs_reciprocal_sqrt, bias=0.25)
+            nc.vector.tensor_tensor(zf[:, t, :], yg[t][:].indirect(n2_t[:]), dw[t][:, S:], ALU.mult)
+        for t in range(PACK):
+            nc.scalar.copy(dw[t][:, :S], d_ps[t][:])
+        zb = tile("zb", [P, PACK * S], BF16, tag="zb")
+        weave(nc.scalar.copy, zb[:], zf[:])
+        zq = tile("zq", [P, S], U32)
+        zs = tile("zs", [P, S], U8)
+        dg = [tile(f"dg{t}", [P, S], F32) for t in range(PACK - 1)]
+        for t in range(PACK - 1):
+            nc.vector.tensor_copy(dg[t][:], dw[t][:].indirect(n4_t[:]))
+        nc.vector.quantize_mx(out=zq[:].bitcast(FP8X4), scales=zs[:], in_=zb[:])
+        dg.append(tile("dg3", [P, S], F32, tag="zb"))
+        nc.vector.tensor_copy(dg[3][:], dw[3][:].indirect(n4_t[:]))
+
+        h_ps = [ps.tile([P, S], F32, name=f"h{t}", tag=f"yh{t}") for t in range(PACK)]
+        hw = [tile(f"hw{t}", [P, S], F32) for t in range(PACK)]
+        big = tile("big", [P, PACK, S], F32)
+        for t in range(PACK):
+            product(h_ps[t][:], w2, t, zq[:], zs[:])
+        for t in range(PACK):
+            nc.scalar.copy(hw[t][:], h_ps[t][:])
+            nc.vector.tensor_tensor(big[:, t, :], h_ps[t][:], dg[t][:], ALU.max)
+
+        oq = tile("oq", [P, S], U32)
+        osc = tile("osc", [P, S], U8)
+        out_rows = out_0.rearrange("(p t) j -> p t j", t=PACK)
+        out_words = out_1[0].rearrange("p c r -> p (c r)").bitcast(I32)
+        for i, (a, b) in enumerate(PIECES):
+            w = b - a
+            last = i == len(PIECES) - 1
+            hg = tile(f"hg{i}", [P, PACK, w], F32, tag="hg")
+            small = tile(f"small{i}", [P, PACK, w], F32)
+            res = tile(f"res{i}", [P, PACK, w], F32)
+            rb = tile(f"rb{i}", [P, PACK * w], BF16)
+            for t in range(PACK):
+                nc.vector.tensor_copy(hg[:, t, :], hw[t][:].indirect(n3_t[:, a // 16 : b // 16]))
+            for t in range(PACK):
+                nc.vector.tensor_tensor(small[:, t, :], d_ps[t][:, a:b], hg[:, t, :], ALU.min)
+            nc.vector.tensor_tensor(res[:], big[:, :, a:b], small[:], ALU.subtract)
+            nc.sync.dma_start(out_rows[:, :, a:b], res[:])
+            weave(nc.vector.tensor_copy if last else nc.scalar.copy, rb[:], res[:])
+            nc.vector.quantize_mx(out=oq[:, a:b].bitcast(FP8X4), scales=osc[:, a:b], in_=rb[:])
+            nc.sync.dma_start(out_words[:, a:b], oq[:, a:b].bitcast(I32))
+        for q in range(4):
+            queue = nc.scalar if q % 2 == 0 else nc.sync
+            queue.dma_start(out_2[0, 4 * q : 4 * q + 4, :].bitcast(I32), osc[32 * q : 32 * q + 4, :].bitcast(I32))

@@ -50,10 +50,10 @@ def tile_picked_latemaxbrms_none_po_kernel(tc, x_words, x_scales, w1_words, w1_s
             nc.sync.dma_start(t[:].bitcast(I32), src[0].bitcast(I32))
             return t
 
-        def deal(name, words, scales):
+        def deal(name, words, scales, engine):
             dw = tile(name + "_dw", [P, 2 * N], U8)
             ds = tile(name + "_ds", [P, N], U8)
-            nc.vector.tensor_copy(dw[:].rearrange("p (t m b) -> p t m b", t=PACK, b=2), words[:].rearrange("p (m t b) -> p t m b", t=PACK, b=2))
+            engine.tensor_copy(dw[:].rearrange("p (t m b) -> p t m b", t=PACK, b=2), words[:].rearrange("p (m t b) -> p t m b", t=PACK, b=2))
             nc.vector.tensor_copy(ds[:].rearrange("p (t m) -> p t m", t=PACK), scales[:].rearrange("p (m t) -> p t m", t=PACK))
             return dw, ds
 
@@ -98,33 +98,34 @@ def tile_picked_latemaxbrms_none_po_kernel(tc, x_words, x_scales, w1_words, w1_s
         n4_t = load_list("n4", n4)
         n3_t = load_list("n3", n3)
 
-        def pick(name, table, dtype, lst):
-            picked = tile(name, [P, S], dtype)
+        def pick(name, table, dtype, lst, tag=None):
+            picked = tile(name, [P, S], dtype, tag=tag)
             nc.vector.tensor_copy(picked[:], table.indirect(lst[:]))
             return picked
 
         xa_s = pick("xa_s", xs[:], U8, offs_t)
-        w1 = deal("w1", w1w, w1s)
+        w1 = deal("w1", w1w, w1s, nc.vector)
         xa_w = pick("xa_w", xw[:].bitcast(U32), U32, offs_t)
         y_ps = [ps.tile([P, S], F32, name=f"y{t}", tag=f"yh{t}") for t in range(PACK)]
         for t in range(PACK):
             product(y_ps[t][:], w1, t, xa_w[:], xa_s[:])
         xb_s = pick("xb_s", xs[:], U8, two_t)
-        xb_w = pick("xb_w", xw[:].bitcast(U32), U32, two_t)
-        w3 = deal("w3", w3w, w3s)
-        w2 = deal("w2", w2w, w2s)
+        xb_w = pick("xb_w", xw[:].bitcast(U32), U32, two_t, tag="w1s")
+        w3 = deal("w3", w3w, w3s, nc.gpsimd)
+        w2 = deal("w2", w2w, w2s, nc.gpsimd)
         d_ps = [ps.tile([P, S], F32, name=f"d{t}") for t in range(PACK)]
         for t in range(PACK):
             product(d_ps[t][:], w3, t, xb_w[:], xb_s[:])
 
         sq = [tile(f"sq{t}", [P, 2 * S], F32) for t in range(PACK)]
+        sq2 = tile("sqcopy", [P, PACK, S], F32)
         yg = [tile(f"yg{t}", [P, 2 * S], F32) for t in range(PACK)]
         dw = [tile(f"dw{t}", [P, 2 * S], F32) for t in range(PACK)]
         for t in range(PACK):
             nc.scalar.activation(sq[t][:, :S], y_ps[t][:], ACT.Square)
-            nc.scalar.activation(sq[t ^ 1][:, S:], y_ps[t][:], ACT.Square)
+            nc.scalar.activation(sq2[:, t, :], y_ps[t][:], ACT.Square)
         for t in range(PACK):
-            nc.vector.tensor_tensor(yg[t][:, S:], sq[t][:].indirect(n1_t[:]), sq[t ^ 1][:, S:], ALU.add)
+            nc.vector.tensor_tensor(yg[t][:, S:], sq[t][:].indirect(n1_t[:]), sq2[:, t, :], ALU.add)
         zf = tile("zf", [P, PACK, S], F32)
         for t in range(PACK):
             nc.scalar.activation(yg[t][:, :S], y_ps[t][:], ACT.Copy, scale=gain[:, t : t + 1])
@@ -150,7 +151,7 @@ def tile_picked_latemaxbrms_none_po_kernel(tc, x_words, x_scales, w1_words, w1_s
             product(h_ps[t][:], w2, t, zq[:], zs[:])
         for t in range(PACK):
             nc.scalar.copy(hw[t][:], h_ps[t][:])
-            nc.vector.tensor_tensor(big[:, t, :], h_ps[t][:], dg[t][:], ALU.max)
+            nc.vector.tensor_tensor(big[:, t, :256], h_ps[t][:, :256], dg[t][:, :256], ALU.max)
 
         oq = tile("oq", [P, S], U32)
         osc = tile("osc", [P, S], U8)
@@ -167,7 +168,14 @@ def tile_picked_latemaxbrms_none_po_kernel(tc, x_words, x_scales, w1_words, w1_s
                 nc.vector.tensor_copy(hg[:, t, :], hw[t][:].indirect(n3_t[:, a // 16 : b // 16]))
             for t in range(PACK):
                 nc.vector.tensor_tensor(small[:, t, :], d_ps[t][:, a:b], hg[:, t, :], ALU.min)
-            nc.vector.tensor_tensor(res[:], big[:, :, a:b], small[:], ALU.subtract)
+            if last:
+                nc.vector.tensor_tensor(res[:], big[:, :, a:b], small[:], ALU.subtract)
+            else:
+                for u in (slice(0, 2), slice(2, 4)):
+                    nc.gpsimd.tensor_tensor(res[:, u, :], big[:, u, a:b], small[:, u, :], ALU.subtract)
+            if i == 0:
+                for t in range(PACK):
+                    nc.vector.tensor_tensor(big[:, t, 256:], h_ps[t][:, 256:], dg[t][:, 256:], ALU.max)
             nc.sync.dma_start(out_rows[:, :, a:b], res[:])
             weave(nc.vector.tensor_copy if last else nc.scalar.copy, rb[:], res[:])
             nc.vector.quantize_mx(out=oq[:, a:b].bitcast(FP8X4), scales=osc[:, a:b], in_=rb[:])

@@ -50,11 +50,11 @@ def tile_picked_latemaxbrms_none_po_kernel(tc, x_words, x_scales, w1_words, w1_s
             nc.sync.dma_start(t[:].bitcast(I32), src[0].bitcast(I32))
             return t
 
-        def deal(name, words, scales, engine):
+        def deal(name, words, scales):
             dw = tile(name + "_dw", [P, 2 * N], U8)
             ds = tile(name + "_ds", [P, N], U8)
-            engine.tensor_copy(dw[:].rearrange("p (t m b) -> p t m b", t=PACK, b=2), words[:].rearrange("p (m t b) -> p t m b", t=PACK, b=2))
-            nc.vector.tensor_copy(ds[:].rearrange("p (t m) -> p t m", t=PACK), scales[:].rearrange("p (m t) -> p t m", t=PACK))
+            nc.gpsimd.tensor_copy(dw[:].rearrange("p (t m b) -> p t m b", t=PACK, b=2), words[:].rearrange("p (m t b) -> p t m b", t=PACK, b=2))
+            nc.gpsimd.tensor_copy(ds[:].rearrange("p (t m) -> p t m", t=PACK), scales[:].rearrange("p (m t) -> p t m", t=PACK))
             return dw, ds
 
         def product(bank, w, t, codes, scales):
@@ -73,20 +73,20 @@ def tile_picked_latemaxbrms_none_po_kernel(tc, x_words, x_scales, w1_words, w1_s
             copy(dst.rearrange("p (c i t) -> p c t i", i=4, t=PACK), src.rearrange("p t (c i) -> p c t i", i=4))
 
         xs = scale_tile("xs", T, nc.gpsimd)
-        w1s = scale_tile("w1s", N, nc.vector)
-        w3s = scale_tile("w3s", N, nc.vector)
-        w2s = scale_tile("w2s", N, nc.vector)
+        w1s = scale_tile("w1s", N, nc.gpsimd)
+        w3s = scale_tile("w3s", N, nc.gpsimd)
+        w2s = scale_tile("w2s", N, nc.gpsimd)
         warm = tile("warm", [P, 2], F32)
         nc.gpsimd.memset(warm[:, 0:1], 1.0)
         nc.scalar.activation(warm[:, 1:2], warm[:, 0:1], ACT.Abs_reciprocal_sqrt)
 
         offs_t = load_list("offs", offs)
-        two_t = load_list("two", two)
         w1w = load_words("w1w", w1_words)
         load_scale_rows(xs, x_scales)
         xw = tile("xw", [P, T], I32)
         nc.sync.dma_start(xw[:], x_words[0].rearrange("p n t -> p (n t)").bitcast(I32))
         load_scale_rows(w1s, w1_scales)
+        two_t = load_list("two", two)
         w3w = load_words("w3w", w3_words)
         w2w = load_words("w2w", w2_words)
         n1_t = load_list("n1", n1)
@@ -104,15 +104,15 @@ def tile_picked_latemaxbrms_none_po_kernel(tc, x_words, x_scales, w1_words, w1_s
             return picked
 
         xa_s = pick("xa_s", xs[:], U8, offs_t)
-        w1 = deal("w1", w1w, w1s, nc.vector)
+        w1 = deal("w1", w1w, w1s)
         xa_w = pick("xa_w", xw[:].bitcast(U32), U32, offs_t)
         y_ps = [ps.tile([P, S], F32, name=f"y{t}", tag=f"yh{t}") for t in range(PACK)]
         for t in range(PACK):
             product(y_ps[t][:], w1, t, xa_w[:], xa_s[:])
         xb_s = pick("xb_s", xs[:], U8, two_t)
-        xb_w = pick("xb_w", xw[:].bitcast(U32), U32, two_t, tag="w1s")
-        w3 = deal("w3", w3w, w3s, nc.gpsimd)
-        w2 = deal("w2", w2w, w2s, nc.gpsimd)
+        xb_w = pick("xb_w", xw[:].bitcast(U32), U32, two_t)
+        w3 = deal("w3", w3w, w3s)
+        w2 = deal("w2", w2w, w2s)
         d_ps = [ps.tile([P, S], F32, name=f"d{t}") for t in range(PACK)]
         for t in range(PACK):
             product(d_ps[t][:], w3, t, xb_w[:], xb_s[:])

from contextlib import ExitStack

import concourse.mybir as mybir

K, T, S, N, H = 512, 2048, 512, 512, 512
FLOPS = 3 * 2 * 512 * 512 * 512

F32 = mybir.dt.float32
BF16 = mybir.dt.bfloat16
I32 = mybir.dt.int32
U32 = mybir.dt.uint32
U16 = mybir.dt.uint16
U8 = mybir.dt.uint8
FP8X4 = mybir.dt.float8_e4m3fn_x4
FP4X4 = mybir.dt.float4_e2m1fn_x4
ALU = mybir.AluOpType
ACT = mybir.ActivationFunctionType

P = 128
PACK = 4
PIECES = ((0, 256), (256, 384), (384, 512))


def tile_picked_latemaxbrms_none_po_kernel(tc, x_words, x_scales, w1_words, w1_scales, gn, w2_words, w2_scales, w3_words, w3_scales, offs, n1, n2, two, n3, n4, out_0, out_1, out_2):
    nc = tc.nc
    with ExitStack() as ctx:
        lists = ctx.enter_context(tc.tile_pool(name="lists", bufs=1))
        sb = ctx.enter_context(tc.tile_pool(name="sb", bufs=1))
        ps = ctx.enter_context(tc.psum_pool(name="ps", bufs=1))

        def tile(name, shape, dtype, tag=None):
            return sb.tile(shape, dtype, name=name, tag=tag or name, align_bytes=64)

        def load_list(name, src):
            t = lists.tile([P, S // 16], U16, name=name)
            nc.sync.dma_start(t[:], src)
            return t

        def scale_tile(name, width, engine):
            t = tile(name, [P, width], U8)
            engine.memset(t[:].bitcast(I32), 0)
            return t

        def load_scale_rows(t, src):
            for q in range(4):
                nc.sync.dma_start(t[32 * q : 32 * q + 4, :].bitcast(I32), src[0, 4 * q : 4 * q + 4, :].bitcast(I32))

        def load_words(name, src):
            t = tile(name, [P, 2 * N], U8)
            nc.sync.dma_start(t[:].bitcast(I32), src[0].bitcast(I32))
            return t

        def deal(name, words, scales):
            dw = tile(name + "_dw", [P, 2 * N], U8)
            ds = tile(name + "_ds", [P, N], U8)
            nc.gpsimd.tensor_copy(dw[:].rearrange("p (t m b) -> p t m b", t=PACK, b=2), words[:].rearrange("p (m t b) -> p t m b", t=PACK, b=2))
            nc.gpsimd.tensor_copy(ds[:].rearrange("p (t m) -> p t m", t=PACK), scales[:].rearrange("p (m t) -> p t m", t=PACK))
            return dw, ds

        def product(bank, w, t, codes, scales):
            dw, ds = w
            nc.tensor.matmul_mx(
                out=bank,
                lhsT=dw[:, 2 * P * t : 2 * P * (t + 1)].bitcast(FP4X4),
                lhsT_scale=ds[:, P * t : P * (t + 1)],
                rhs=codes.bitcast(FP8X4),
                rhs_scale=scales,
                start=True,
                stop=True,
            )

        def weave(copy, dst, src):
            copy(dst.rearrange("p (c i t) -> p c t i", i=4, t=PACK), src.rearrange("p t (c i) -> p c t i", i=4))

        xs = scale_tile("xs", T, nc.gpsimd)
        w1s = scale_tile("w1s", N, nc.gpsimd)
        w3s = scale_tile("w3s", N, nc.gpsimd)
        w2s = scale_tile("w2s", N, nc.gpsimd)
        warm = tile("warm", [P, 2], F32)
        nc.gpsimd.memset(warm[:, 0:1], 1.0)
        nc.scalar.activation(warm[:, 1:2], warm[:, 0:1], ACT.Abs_reciprocal_sqrt)

        offs_t = load_list("offs", offs)
        w1w = load_words("w1w", w1_words)
        load_scale_rows(xs, x_scales)
        xw = tile("xw", [P, T], I32)
        nc.sync.dma_start(xw[:], x_words[0].rearrange("p n t -> p (n t)").bitcast(I32))
        load_scale_rows(w1s, w1_scales)
        two_t = load_list("two", two)
        w3w = load_words("w3w", w3_words)
        w2w = load_words("w2w", w2_words)
        n1_t = load_list("n1", n1)
        load_scale_rows(w3s, w3_scales)
        gain = tile("gain", [P, PACK], F32)
        nc.sync.dma_start(gain[:], gn.rearrange("(p t) o -> p (t o)", t=PACK))
        n2_t = load_list("n2", n2)
        load_scale_rows(w2s, w2_scales)
        n4_t = load_list("n4", n4)
        n3_t = load_list("n3", n3)

        def pick(name, table, dtype, lst, tag=None):
            picked = tile(name, [P, S], dtype, tag=tag)
            nc.vector.tensor_copy(picked[:], table.indirect(lst[:]))
            return picked

        xa_s = pick("xa_s", xs[:], U8, offs_t)
        w1 = deal("w1", w1w, w1s)
        xa_w = pick("xa_w", xw[:].bitcast(U32), U32, offs_t)
        y_ps = [ps.tile([P, S], F32, name=f"y{t}", tag=f"yh{t}") for t in range(PACK)]
        for t in range(PACK):
            product(y_ps[t][:], w1, t, xa_w[:], xa_s[:])
        xb_s = pick("xb_s", xs[:], U8, two_t)
        xb_w = pick("xb_w", xw[:].bitcast(U32), U32, two_t)
        w3 = deal("w3", w3w, w3s)
        w2 = deal("w2", w2w, w2s)
        d_ps = [ps.tile([P, S], F32, name=f"d{t}") for t in range(PACK)]
        for t in range(PACK):
            product(d_ps[t][:], w3, t, xb_w[:], xb_s[:])

        sq = [tile(f"sq{t}", [P, 2 * S], F32) for t in range(PACK)]
        sq2 = tile("sqcopy", [P, PACK, S], F32)
        yg = [tile(f"yg{t}", [P, 2 * S], F32) for t in range(PACK)]
        dw = [tile(f"dw{t}", [P, 2 * S], F32) for t in range(PACK)]
        for t in range(PACK):
            nc.scalar.activation(sq[t][:, :S], y_ps[t][:], ACT.Square)
            nc.scalar.activation(sq2[:, t, :], y_ps[t][:], ACT.Square)
        for t in range(PACK):
            nc.vector.tensor_tensor(yg[t][:, S:], sq[t][:].indirect(n1_t[:]), sq2[:, t, :], ALU.add)
        zf = tile("zf", [P, PACK, S], F32)
        for t in range(PACK):
            nc.scalar.activation(yg[t][:, :S], y_ps[t][:], ACT.Copy, scale=gain[:, t : t + 1])
            nc.scalar.activation(dw[t][:, S:], yg[t][:, S:], ACT.Abs_reciprocal_sqrt, bias=0.25)
            nc.vector.tensor_tensor(zf[:, t, :], yg[t][:].indirect(n2_t[:]), dw[t][:, S:], ALU.mult)
        for t in range(PACK):
            nc.scalar.copy(dw[t][:, :S], d_ps[t][:])
        zb = tile("zb", [P, PACK * S], BF16, tag="zb")
        weave(nc.scalar.copy, zb[:], zf[:])
        zq = tile("zq", [P, S], U32)
        zs = tile("zs", [P, S], U8)
        dg = [tile(f"dg{t}", [P, S], F32) for t in range(PACK - 1)]
        for t in range(PACK - 1):
            nc.vector.tensor_copy(dg[t][:], dw[t][:].indirect(n4_t[:]))
        nc.vector.quantize_mx(out=zq[:].bitcast(FP8X4), scales=zs[:], in_=zb[:])
        dg.append(tile("dg3", [P, S], F32, tag="zb"))
        nc.vector.tensor_copy(dg[3][:], dw[3][:].indirect(n4_t[:]))

        h_ps = [ps.tile([P, S], F32, name=f"h{t}", tag=f"yh{t}") for t in range(PACK)]
        hw = [tile(f"hw{t}", [P, S], F32) for t in range(PACK)]
        big = tile("big", [P, PACK, S], F32)
        for t in range(PACK):
            product(h_ps[t][:], w2, t, zq[:], zs[:])
        for t in range(PACK):
            nc.scalar.copy(hw[t][:], h_ps[t][:])
            nc.vector.tensor_tensor(big[:, t, :256], h_ps[t][:, :256], dg[t][:, :256], ALU.max)

        oq = tile("oq", [P, S], U32)
        osc = tile("osc", [P, S], U8)
        out_rows = out_0.rearrange("(p t) j -> p t j", t=PACK)
        out_words = out_1[0].rearrange("p c r -> p (c r)").bitcast(I32)
        for i, (a, b) in enumerate(PIECES):
            w = b - a
            last = i == len(PIECES) - 1
            hg = tile(f"hg{i}", [P, PACK, w], F32, tag="hg")
            small = tile(f"small{i}", [P, PACK, w], F32)
            res = tile(f"res{i}", [P, PACK, w], F32)
            rb = tile(f"rb{i}", [P, PACK * w], BF16)
            for t in range(PACK):
                nc.vector.tensor_copy(hg[:, t, :], hw[t][:].indirect(n3_t[:, a // 16 : b // 16]))
            for t in range(PACK):
                nc.vector.tensor_tensor(small[:, t, :], d_ps[t][:, a:b], hg[:, t, :], ALU.min)
            if last:
                nc.vector.tensor_tensor(res[:], big[:, :, a:b], small[:], ALU.subtract)
            else:
                for u in (slice(0, 2), slice(2, 4)):
                    nc.gpsimd.tensor_tensor(res[:, u, :], big[:, u, a:b], small[:, u, :], ALU.subtract)
            if i == 0:
                for t in range(PACK):
                    nc.vector.tensor_tensor(big[:, t, 256:], h_ps[t][:, 256:], dg[t][:, 256:], ALU.max)
            nc.sync.dma_start(out_rows[:, :, a:b], res[:])
            weave(nc.vector.tensor_copy if last else nc.scalar.copy, rb[:], res[:])
            nc.vector.quantize_mx(out=oq[:, a:b].bitcast(FP8X4), scales=osc[:, a:b], in_=rb[:])
            nc.sync.dma_start(out_words[:, a:b], oq[:, a:b].bitcast(I32))
        for q in range(4):
            queue = nc.scalar if q % 2 == 0 else nc.sync
            queue.dma_start(out_2[0, 4 * q : 4 * q + 4, :].bitcast(I32), osc[32 * q : 32 * q + 4, :].bitcast(I32))
